import numpy as np, ml_dtypes
CORES = [25,29,65,69,153,157,193,197]
N = 8
BF = ml_dtypes.bfloat16
def gentries(a):
    return np.ascontiguousarray(a.reshape(8, 16, -1).transpose(0, 2, 1)).reshape(8, -1)
def gtable(e):
    e = np.asarray(e); return np.ascontiguousarray(e.reshape(8, -1, 16).transpose(0, 2, 1)).reshape(128, -1).astype(np.int32)
W, S, L, RO, RW, BC, BR = 2048, 8, 256, 3, 1, 3, 4
def people(rng, street, fame, one):
    sh = (N, 8, 16, W); col = np.arange(W) % S
    a = np.where(rng.random(sh) < street, S * rng.integers(0, L, sh) + col, rng.integers(0, W, sh))
    st = rng.integers(0, L, (N * 8, 24)); star = S * np.take_along_axis(st, rng.integers(0, 24, (N * 8, 16 * W)), 1).reshape(sh) + col
    a = np.where(rng.random(sh) < fame, star, a)
    return np.where(rng.random((N, 8, 1, W)) < one, a[:, :, :1], a)
def strangers(rng, *sh):
    return S * rng.integers(0, L, sh + (W,)) + (np.arange(W) + rng.integers(1, S, sh + (W,))) % S
def pack(x, a, tt):
    return {"x": np.ascontiguousarray(np.reshape(x, (N, 128, W))).astype(np.float32).astype(BF), "aq": np.ascontiguousarray(np.reshape(a, (N, 128, W))).astype(np.int32),
            "tg": np.stack([gtable(b) for b in tt])}
def mixed(rng):
    return people(rng, rng.choice(np.array([0.3, 0.5, 0.7]), (N, 8, 1, 1)), rng.choice(np.array([0.0, 0.05, 0.15]), (N, 8, 1, 1)), 0.02)
def setup_inputs(rng):
    return pack(rng.integers(0, 256, (N, 8, 16, W)), mixed(rng), rng.integers(0, W, (N, 8, W)))
def setup_inputs_ties(rng):
    x = 127 * rng.integers(0, 3, (N, 8, 16, W)); a = mixed(rng)
    x[:, 0] = 255 * rng.integers(0, 2, (N, 1, W)); x[:, 1] = rng.integers(0, 2, (N, 16, W)); x[:, 3] = rng.integers(0, 256, (N, 16, 1))
    x[:, 5] = rng.integers(0, 256, (16, 4))[:, rng.integers(0, 4, (N, W))].transpose(1, 0, 2)
    a[:, 6, 8:] = a[:, 6, :8]; a[:, 7, 1:] = a[:, 7, :15]
    return pack(x, a, rng.integers(0, W, (N, 8, W)))
def setup_inputs_stars(rng):
    a = np.zeros((N, 8, 16, W), np.int64); ev = a[:, ::2].shape
    a[:, ::2] = S * rng.choice(np.array([0, 1, 2, 3, 4, 5, L - 8, L - 1]), ev) + np.arange(W) % S
    a[:, 1::2] = rng.choice(np.array([0, 1, W // 2, W - 2, W - 1]), ev)
    a = np.where(rng.random((N, 8, 1, W)) < 0.2, a[:, :, :1], a)
    return pack(rng.integers(0, 256, (N, 8, 16, W)), a, rng.choice(np.array([0, 1, W // 2, W - 2, W - 1, W // 4]), (N, 8, W)))
def setup_inputs_free(rng):
    a = mixed(rng); a[:, ::2] = strangers(rng, N, 4, 16)
    x = rng.integers(0, 256, (N, 8, 16, W)); x[:, :4] = x[:, :4] & 1; x[:, 4:6] = x[:, 4:6] & 63
    share = np.zeros((N, 6, 1, 1)); share[1::2, :2] = 1.0; share[:, 2:4] = 0.5; share[:, 4:6] = 0.03
    x[:, :6] = np.where(rng.random((N, 6, 1, W)) < share, 255 - x[:, :6], x[:, :6])
    return pack(x, a, rng.integers(0, W, (N, 8, W)))
def setup_inputs_chains(rng):
    a = mixed(rng); a[:, ::2] = strangers(rng, N, 4, 16)
    i = np.arange(L); bl = i[(i % 8 > RW) & (i % 8 <= RW + BC)]; n = len(bl)
    for q in range(N):
        for g in range(8):
            for t in range(RO):
                o = rng.permutation(bl); c = rng.integers(0, 6, n)
                nx = np.where(c == 0, rng.integers(0, L, n), np.where(c == 1, o, np.roll(o, -1)))
                nx[0] = o[0]; nx[1] = o[2]; nx[2] = o[1]; nx[3:10] = o[4:11]
                town = a[q, g]; town[:, S * o + t] = S * nx + t
    return pack(rng.integers(0, 256, (N, 8, 16, W)), a, rng.integers(0, W, (N, 8, W)))
def setup_inputs_spread(rng):
    x = np.minimum((np.exp2(8 * rng.random((N, 8, 1, W))) * rng.random((N, 8, 16, W))).astype(np.int64), 255)
    e = rng.choice(np.array([1.0, 2.0, 4.0]), (N, 8, 1, 1)); sh = (N, 8, 16, W)
    a = np.minimum((W * np.power(rng.random(sh), e)).astype(np.int64), W - 1)
    s = S * np.minimum((L * np.power(rng.random(sh), e)).astype(np.int64), L - 1) + np.arange(W) % S
    a = np.where(rng.random(sh) < rng.random((N, 8, 1, 1)), s, a)
    return pack(x, a, np.minimum((W * np.power(rng.random((N, 8, W)), e[:, :, 0])).astype(np.int64), W - 1))
def check_inputs(d):
    bad = []; xf = np.asarray(d["x"]).astype(np.float32)
    if not np.all((xf >= 0) & (xf <= 255) & (xf == np.floor(xf))): bad.append("whole numbers and range of x")
    for k in ("aq", "tg"):
        if np.min(d[k]) < 0 or np.max(d[k]) > W - 1: bad.append("range of " + k)
    return bad
def reference(x, aq, tg):
    xs = x.astype(np.float32).astype(np.int32).reshape(N, 8, 16, W); aw = aq.astype(np.int64).reshape(N, 8, 16, W)
    tt = np.stack([gentries(a) for a in tg]).astype(np.int64)
    lane = np.arange(L); role = lane % 8; ri = np.arange(N)[:, None]; gi = np.arange(8)[None, :]
    blk = (role > RW) & (role <= RW + BC)
    yx = np.zeros((N, 8, 16, RO, L), np.float32); ym = np.zeros((N, 8, RO, L), np.float32)
    for t in range(RO):
        v = S * lane + t; xv = xs[..., v]; own = aw[..., v]
        near = np.take_along_axis(xs, own.reshape(N, 8, 1, 16 * L), 3).reshape(N, 8, 16, 16, L)
        c = np.add.reduce(np.abs(near - xv[:, :, :, None, :]), axis=2); k = np.argmax(c, axis=2)
        tt[:, :, v] = np.take_along_axis(own, k[:, :, None, :], 2)[:, :, 0]
        uu = np.take_along_axis(own, ((k + 1) % 16)[:, :, None, :], 2)[:, :, 0]
        p = tt[:, :, v][..., 0::8]; o = uu[..., 0::8]; D = p.shape[-1]
        meet = (p[..., None] == p[:, :, None, :]) | (p[..., None] == o[:, :, None, :]) | (o[..., None] == p[:, :, None, :]) | (o[..., None] == o[:, :, None, :])
        void = (p == o) | np.any(meet & (np.tri(D, D, -1) > 0), axis=-1)
        s = np.zeros((N, 8, W), np.int64) + np.arange(W)
        q, g, i = np.nonzero(~void); s[q, g, p[q, g, i]] = o[q, g, i]; s[q, g, o[q, g, i]] = p[q, g, i]
        tt = np.take_along_axis(s, tt, 2); uu = np.take_along_axis(s, uu, 2)
        for w in range(1, RW + 1):
            place = tt[:, :, v][..., w::8]; val = uu[..., w::8]
            for i in range(place.shape[-1] - 1, -1, -1):
                tt[ri, gi, place[..., i]] = val[..., i]
        tv = tt[:, :, v]; bt = tv[..., blk]; b = np.zeros((N, 8, W), bool)
        for rnd in range(BR):
            q, g, i = np.nonzero(~b[:, :, v[blk]]); b = np.zeros((N, 8, W), bool); b[q, g, bt[q, g, i]] = True
        free = ~b[:, :, v]
        nx = []; nm = []
        for r in range(N):
            h = (r + 1 + t % (N - 1)) % N; a = tv[r]
            al = np.take_along_axis(aw[h], a[:, None, :], 2)
            far = np.take_along_axis(xs[h], al.reshape(8, 1, 16 * L), 2).reshape(8, 16, 16, L)
            e = np.add.reduce(np.abs(far - xv[r][:, :, None, :]), axis=1); k = np.argmin(e, axis=1)
            m = np.take_along_axis(al, k[:, None, :], 1)[:, 0]; xa = np.take_along_axis(xs[h], a[:, None, :], 2)
            nx.append(np.where(free[r][:, None, :], (xv[r] + xa) >> 1, xv[r])); nm.append(np.where(free[r], m, own[r, :, t]))
        nx = np.stack(nx); nm = np.stack(nm)
        xs[..., v] = nx; aw[:, :, t, v] = nm; yx[:, :, :, t] = nx; ym[:, :, t] = nm
    return {"yx": yx.reshape(N, 128, RO * L).astype(BF), "ym": ym.reshape(N, 8, RO * L).astype(np.float32), "yt": tt.astype(np.float32)}

from concourse.bass import DstId, RemoteDMATransfer
from concourse.mybir import AluOpType as A, AxisListType, ActivationFunctionType as F

N, RO, WT = 8, 3, 2144
f32, bf, i32, u16, f16 = "float32", "bfloat16", "int32", "uint16", "float16"


def _sb(n, d):
    return ("sbuf", [128, n], d)


SCRATCH = {
    "xo": _sb(2048, bf), "ao": _sb(2048, i32), "tgi": _sb(128, i32), "tgu": _sb(128, u16),
    "pid": _sb(8, i32), "cf": _sb(40, f32), "yrow": _sb(256, f32), "y16": _sb(128, f32), "jrow": _sb(16, f32),
    "ival": _sb(256, bf), "tb": _sb(256, bf), "tbm": _sb(512, bf), "zp": _sb(144, bf), "zm": _sb(144, bf), "z1": _sb(144, f16),
    "zk": _sb(288, f16), "bo": _sb(128, f16), "idp": _sb(128, bf), "idm": _sb(128, bf), "dg": _sb(384, f16), "selp": _sb(8, f32),
    "rst": _sb(256, f32), "keep": _sb(256, f32), "mk": _sb(32, f32), "oht": _sb(16, f32), "ohu": _sb(16, f32),
    "prm": _sb(320, bf), "dm": _sb(8, f32), "cz": _sb(240, bf), "one": _sb(2, bf),
    "nl": _sb(48, u16), "jl": _sb(48, u16), "jn": _sb(16, u16), "tlc": _sb(16, u16),
    "xvn": _sb(768, bf), "xvj": _sb(768, bf), "ownn": _sb(768, u16), "ownj": _sb(768, f16),
    "dvc": _sb(4096, bf), "abc": _sb(4096, bf), "dvv": _sb(4096, bf), "abv": _sb(4096, bf),
    "ksc": _sb(256, f32), "kic": _sb(32, i32), "kuc": _sb(16, u16),
    "ksv": _sb(256, f32), "kiv": _sb(32, i32), "kuv": _sb(16, u16),
    "mp": _sb(320, f16), "mpm": _sb(256, f16), "ee": _sb(320, f32), "pen": _sb(4, f32),
    "tl": _sb(60, u16), "sl": _sb(12, u16), "rl": _sb(2, u16), "zl": _sb(12, u16), "al": _sb(48, u16),
    "vs": _sb(128, f32), "zz": _sb(128, f32), "su": _sb(96, f32), "wt": _sb(WT, f32), "wm": _sb(512, f32),
    "dd": _sb(512, i32), "fr": _sb(768, bf), "fd": _sb(256, bf), "am": _sb(2048, bf), "nb": _sb(8, bf),
    "nbx": _sb(1024, bf), "alj": _sb(256, f32), "alu": _sb(256, u16), "alf": _sb(256, f16), "lu": _sb(16, u16),
    "ld": _sb(512, bf), "dmv": _sb(256, f32),
    "ytw": _sb(WT, f32), "yv": _sb(512, f32), "yr": _sb(64, f32), "yc": _sb(64, f32),
}
BANKS = ("pdc", "pdv", "ps0", "ps1", "pr", "pb", "pq", "pk")
for _b in BANKS:
    SCRATCH[_b] = ("psum", [128, 512], f32)
for _t in range(RO):
    SCRATCH["xh%d" % _t] = _sb(2048, bf)
    SCRATCH["ah%d" % _t] = _sb(2048, i32)
    SCRATCH["xr%d" % _t] = _sb(4096, bf)
    SCRATCH["st%d" % _t] = _sb(WT, f32)
    SCRATCH["zt%d" % _t] = _sb(WT, f32)
    SCRATCH["nx%d" % _t] = _sb(256, bf)
    SCRATCH["no%d" % _t] = _sb(256, f32)
UPD = [(0, 1), (0, 2), (1, 2)]
for _a, _b in UPD:
    SCRATCH["ux%d%d" % (_a, _b)] = _sb(256, bf)
    SCRATCH["ua%d%d" % (_a, _b)] = _sb(256, f32)
SEMAPHORES = (["qV", "qS", "qP", "qG", "rx", "ra", "rux0", "rux1", "rua0", "rua1"]
              + ["bx%d" % t for t in range(RO)] + ["ba%d" % t for t in range(RO)]
              + ["ux%d%d" % p for p in UPD] + ["ua%d%d" % p for p in UPD] + ["d%d" % k for k in range(40)])

S_CHOICE = ((6, 7), (6, 7), (5, 6, 7))
S_VISIT = ((0, 1, 2, 3, 4, 5, 6, 7), (0, 1, 2, 3, 4, 5), (0, 1, 2))
CY, PCY, GA, SC, SYNC = 1.0e-3, 0.55e-3, 1.56, 3.8, 0.08
LOOK = 0.3
BOOST = {"c1": 9.0, "c2": 10.0, "n0": 5.0, "n1": -8.0, "n2": 8.0, "b0": 7.0, "b1": 22.0, "b2": -10.0, "v0": -3.0, "v1": -2.0,
         "v2": -11.0, "w0": -2.0, "w1": -2.0, "w2": -2.0, "yt": -8.0, "pre": -1.0}
PARTS = ((64, 160), (160, 256), (0, 64))
BULK = ((5.0, 9.0), (14.0, 18.0), (26.0, 28.0))
HOP = 5.0


def bits(m):
    return bin(m).count("1")


def plan(T, topo):
    C = T.cores
    out = {}
    for h in range(N):
        c = C[h]
        dst = [(h - 1 - t % (N - 1)) % N for t in range(RO)]
        far = [t for t in range(RO) if not topo.may_write(c, C[dst[t]])]
        way = {}
        for t in range(RO):
            if C[dst[t]] in topo.cores_of(c):
                way[t] = "direct"
            elif t - 1 in far and way[t - 1] == "relay" and C[dst[t]] in topo.cores_of(C[dst[t - 1]]):
                way[t] = "handed"
            else:
                way[t] = "relay"
        place = [k for k in topo.cores_of(c) if k in C].index(c)
        able = [k for k in topo.cores_of(c) if k not in C and all(topo.may_write(k, C[d]) for d in dst)]
        near = [k for k in able if topo.die(k) == topo.die(c)]
        other = [k for k in able if topo.die(k) != topo.die(c)]
        out[h] = {"dst": dst, "far": far, "way": way, "helpers": [near[place % len(near)], other[place % len(other)]]}
    return out


def halves(topo, src, dsts):
    e = [k for k in topo.engines(src, dsts[0]) if all(k in topo.engines(src, d) for d in dsts)]
    n = len(e) // len(dsts)
    return [sum(1 << k for k in e[i * n:(i + 1) * n]) for i in range(len(dsts))]


def send(g, T, topo, src, items, local):
    ms = halves(topo, src, [i[0] for i in items])
    if len(items) == 1:
        d, o, i, s = items[0]
        rid, pid = topo.addr(d, src)
        g.remote_dma(o, i, T.sem[s], T.sem[local], pid, rid, ms[0])
    else:
        tr = []
        for (d, o, i, s), m in zip(items, ms):
            rid, pid = topo.addr(d, src)
            tr.append(RemoteDMATransfer(dst_ids=[DstId(rid=rid, pnc=pid)], dma_engine_mask=m, remote_sem=T.sem[s], src=i, dst=o))
        g.remote_dma_fused(tr, local_sem=T.sem[local])


def upd_items(T, P, h, a, kind, src_ap):
    own, rel = [], []
    for (a2, b) in UPD:
        if a2 == a:
            nm = "u%s%d%d" % (kind, a, b)
            (rel if b in P[h]["far"] else own).append((T.cores[P[h]["dst"][b]], T[nm][:], src_ap, nm))
    return own, rel


def arrivals(T, topo, P, r):
    C, n = T.cores, {}
    for t in range(RO):
        h = (r + 1 + t % (N - 1)) % N
        w = P[h]["way"][t]
        if w == "direct":
            k = bits(topo.mask(C[h], C[r]))
        elif w == "handed":
            k = bits(topo.mask(C[P[h]["dst"][t - 1]], C[r]))
        else:
            k = sum(bits(topo.mask(e, C[r])) for e in P[h]["helpers"])
        n["bx%d" % t] = n["ba%d" % t] = k
    for (a, b) in UPD:
        h = (r + 1 + b % (N - 1)) % N
        for half, kind in enumerate("xa"):
            own, rel = upd_items(T, P, h, a, kind, None)
            e = P[h]["helpers"][half]
            if b in P[h]["far"]:
                k = bits(halves(topo, e, [i[0] for i in rel])[0])
            else:
                k = bits(halves(topo, C[h], [e] * (1 if rel else 0) + [i[0] for i in own])[0])
            n["u%s%d%d" % (kind, a, b)] = k
    return n


def helper_program(g, core, T, topo, P, h, half):
    C = T.cores
    k = bits(halves(topo, C[h], P[h]["helpers"])[0])
    cols = slice(1024 * half, 1024 * half + 1024)
    total = 0
    for n, t in enumerate(t for t in range(RO) if P[h]["way"][t] == "relay"):
        d = C[P[h]["dst"][t]]
        for kind, src in (("x", T.xo), ("a", T.ao)):
            if n == 0:
                g.wait_ge(T.sem["r" + kind], k)
            elif kind == "x":
                g.wait_ge(T.sem.d0, total)
            send(g, T, topo, core, [(d, T["%sh%d" % (kind, t)][:, cols], src[:, cols], "b%s%d" % (kind, t))], "d0")
            total += bits(topo.mask(core, d))
    kind = "xa"[half]
    for a in range(RO - 1):
        own, rel = upd_items(T, P, h, a, kind, T[("nx%d" if kind == "x" else "no%d") % a][:])
        if rel:
            g.wait_ge(T.sem["ru%s%d" % (kind, a)], bits(halves(topo, C[h], [core] + [i[0] for i in own])[0]))
            send(g, T, topo, core, rel, "d0")
            total += sum(bits(m) for m in halves(topo, core, [i[0] for i in rel]))
    g.wait_ge(T.sem.d0, total)


def build(g, core, T, topo, P, r):
    ops = []
    nd = [0]
    grp = ["pre"]
    C = T.cores
    V, S, PE = g.vector, g.scalar, g.tensor

    def op(eng, fn, rd, wr, cost, **kw):
        o = {"e": eng, "fn": fn, "rd": list(rd), "wr": list(wr), "c": cost, "lat": 0.0, "boost": BOOST.get(grp[0], 0.0), "g": grp[0]}
        o.update(kw)
        ops.append(o)
        return len(ops) - 1

    def vc(n, k=1.0):
        return max(64, n * k) * CY

    def ts(out, in0, s1, s2, o0, o1, rd, wr, n, k=1.0):
        if o1 is None:
            return op("V", lambda: V.tensor_scalar(out, in0, s1, None, o0), rd, wr, vc(n, k))
        return op("V", lambda: V.tensor_scalar(out, in0, s1, s2, o0, o1), rd, wr, vc(n, k))

    def cp(out, in_, rd, wr, n, k=1.0):
        return op("V", lambda: V.tensor_copy(out, in_), rd, wr, vc(n, k))

    def tt(out, a, b, o, rd, wr, n, k=1.0):
        return op("V", lambda: V.tensor_tensor(out, a, b, o), rd, wr, vc(n, k))

    def vg(out, win, off, rd, wr, n, in1=None, o=None):
        if in1 is None:
            return op("V", lambda: V.tensor_copy(out, win.indirect(off)), rd, wr, 0.05 + n * GA * CY)
        return op("V", lambda: V.tensor_tensor(out, win.indirect(off), in1, o), rd, wr, 0.05 + n * GA * CY)

    def vsc(win, off, in_, rd, wr, n):
        return op("V", lambda: V.tensor_copy(win.indirect(off), in_), rd, wr, 0.05 + n * SC * CY)

    def sg(out, win, off, rd, wr, n):
        return op("S", lambda: S.activation(out, win.indirect(off), F.Copy), rd, wr, 0.065 + n * GA * CY)

    def act(out, in_, f, rd, wr, n):
        return op("S", lambda: S.activation(out, in_, f), rd, wr, vc(n))

    def scan(out, d0, d1, o0, o1, rd, wr, n):
        return op("V", lambda: V.tensor_tensor_scan(out, d0, d1, 0.0, o0, o1), rd, wr, vc(n))

    def mm(out, l, rh, st, sp, rd, bank, n, k=1):
        return op("P", lambda: PE.matmul(out, l, rh, st, sp), rd, [bank], max(64, n) * k * PCY)

    def iota(out, pat, base, cm, wr, n, flt=True):
        if flt:
            return op("G", lambda: g.iota(out, pat, base, cm, allow_small_or_imprecise_dtypes=True), [], wr, 0.13 + 2 * n * CY)
        return op("G", lambda: g.iota(out, pat, base, cm), [], wr, 0.13 + 2 * n * CY)

    def gcopy(out, in_, rd, wr):
        return op("G", lambda: g.affine_select(out, in_, [[0, 256]], A.is_gt, 0.0, 1, 0), rd, wr, 0.17 + 512 * CY, boost=50.0)

    def dma(q, out, in_, rd, wr, lat):
        s = "d%d" % nd[0]
        nd[0] += 1
        e = {"Y": g.sync, "S": g.scalar}[q]
        return op(q, lambda: e.dma_start(out, in_).then_inc(T.sem[s], 16), rd, wr, 0.1, lat=lat, sem=(s, 16))

    def rem(items, rd, wr, lat, boost=100.0, **kw):
        s = "d%d" % nd[0]
        nd[0] += 1
        k = sum(bits(m) for m in halves(topo, core, [i[0] for i in items]))
        return op("G", lambda: send(g, T, topo, core, items, s), rd, wr, 0.6, lat=lat, sem=(s, k), boost=boost, **kw)

    arr = arrivals(T, topo, P, r)

    def ext(name, wr, after, lat):
        return op("X", None, [], wr, 0.0, lat=lat, sem=(name, arr[name]), soft=after)

    dma("Y", T.xo[:], T.x[:], [], ["xo"], 3.6)
    dma("S", T.ao[:, 0:1024], T.aq[:, 0:1024], [], ["ao0"], 6.0)
    dma("Y", T.ao[:, 1024:2048], T.aq[:, 1024:2048], [], ["ao1"], 6.5)
    AO = ["ao0", "ao1"]
    dma("Y", T.tgi[:], T.tg[:], [], ["tgi"], 7.0)
    iota(T.pid[:, 0:1], [[0, 1]], 0, 1, ["pid"], 1, False)
    iota(T.yrow[:], [[1, 256]], 0, 0, ["yrow"], 256)
    iota(T.jrow[:], [[8, 8], [1024, 2]], 0, 0, ["jrow"], 16)
    iota(T.tb[:], [[0, 16], [-1, 16]], 15, 0, ["tb"], 256)
    iota(T.y16[:], [[16, 8], [0, 16]], 0, 0, ["y16"], 128)
    iota(T.ival[:], [[1, 8], [8, 32]], 0, 0, ["ival"], 256)
    for o in ops[4:]:
        o["boost"] = 20.0
    pid, cf, y = T.pid, T.cf, T.yrow

    def col(k):
        return cf[:, k:k + 1]
    for k, s in enumerate((15, 1, 14, 7, 8, 112)):
        ts(pid[:, k + 1:k + 2], pid[:, 0:1], s, None, A.bitwise_and, None, ["pid"], ["pi%d" % (k + 1)], 1)
    cp(cf[:, 0:7], pid[:, 0:7], ["pid"] + ["pi%d" % k for k in range(1, 7)], ["cf"], 7)
    ts(col(7), col(2), 1024.0, None, A.mult, None, ["cf"], ["c7"], 1)
    ts(col(8), col(3), 4.0, col(7), A.mult, A.add, ["cf", "c7"], ["c8"], 1)
    ts(cf[:, 9:12], y[:, 0:3], col(8), None, A.add, None, ["yrow", "c8"], ["c9"], 3)
    for t in range(RO):
        ts(T.nl[:, 16 * t:16 * t + 16], y[:, 0:16], 64.0, col(9 + t), A.mult, A.add, ["yrow", "c9"], ["nl%d" % t], 16)
    ts(col(12), col(1), 64.0, None, A.mult, None, ["cf"], ["c12"], 1)
    for t in range(RO):
        ts(T.jl[:, 16 * t:16 * t + 16], T.jrow[:], col(12), float(t), A.add, A.add, ["jrow", "c12"], ["jl%d" % t], 16)
    ts(col(13), col(5), 0.125, None, A.mult, None, ["cf"], ["c13"], 1)
    ts(col(14), col(4), 32.0, col(13), A.mult, A.add, ["cf", "c13"], ["c14"], 1)
    ts(T.jn[:], y[:, 0:16], 2.0, col(14), A.mult, A.add, ["yrow", "c14"], ["jn"], 16)
    ts(col(15), col(1), 16.0, None, A.mult, None, ["cf"], ["c15"], 1)
    ts(T.tlc[:], y[:, 0:16], col(15), None, A.add, None, ["yrow", "c15"], ["tlc"], 16)
    ts(col(16), col(6), 15.0, None, A.add, None, ["cf"], ["c16"], 1)
    for buf, nm, w in ((T.zp, "zp", 16.0), (T.zm, "zm", -16.0), (T.z1, "z1", 1.0)):
        ts(buf[:], y[:, 0:144], col(16), w, A.is_equal, A.mult, ["yrow", "c16"], [nm], 144)
    ts(T.bo[:], T.y16[:], col(6), None, A.is_equal, None, ["y16", "cf"], ["bo"], 128)
    ts(T.idp[:], y[:, 0:128], col(0), None, A.is_equal, None, ["yrow", "cf"], ["idp"], 128)
    ts(T.idm[:], y[:, 0:128], col(0), -1.0, A.is_equal, A.mult, ["yrow", "cf"], ["idm"], 128)
    ts(cf[:, 17:20], y[:, 0:3], col(1), -1.0, A.is_equal, A.mult, ["yrow", "cf"], ["c17"], 3)
    ts(cf[:, 25:27], y[:, 0:2], col(1), None, A.is_equal, None, ["yrow", "cf"], ["c25"], 2)
    for t in range(RO):
        ts(T.dg[:, 128 * t:128 * t + 128], y[:, 0:128], col(0), col(17 + t), A.is_equal, A.mult, ["yrow", "cf", "c17"], ["dg%d" % t], 128)
    for k in range(RO - 1):
        ts(T.zk[:, 144 * k:144 * k + 144], y[:, 0:144], col(16), col(25 + k), A.is_equal, A.mult, ["yrow", "c16", "c25"], ["zk%d" % k], 144)
        ts(T.tbm[:, 256 * k:256 * k + 256], T.tb[:], 15.0 - k, -131072.0, A.is_equal, A.mult, ["tb"], ["tbm%d" % k], 256, 0.5)
    ts(T.selp[:], y[:, 0:128:16], col(0), 0.125, A.is_equal, A.mult, ["yrow", "cf"], ["selp"], 8)
    ts(T.rst[:], T.tb[:], 15.0, -1.0e6, A.is_equal, A.mult, ["tb"], ["rst"], 256)
    ts(T.keep[:], T.tb[:], 15.0, None, A.not_equal, None, ["tb"], ["keep"], 256)
    ts(col(20), col(1), -1.0, 15.0, A.mult, A.add, ["cf"], ["c20"], 1)
    ts(T.mk[:], T.tb[:, 0:32], col(20), None, A.is_equal, None, ["tb", "c20"], ["mk"], 32)
    ts(T.pk[:, 0:256], T.tb[:], col(20), None, A.is_equal, None, ["tb", "c20"], ["pk"], 256)
    ts(T.oht[:], y[:, 0:16], col(20), None, A.is_equal, None, ["yrow", "c20"], ["oht"], 16)
    ts(col(21), col(1), 0.0, -16.0, A.is_equal, A.mult, ["cf"], ["c21"], 1)
    ts(col(22), col(20), 1.0, col(21), A.add, A.add, ["c20", "c21"], ["c22"], 1)
    ts(T.ohu[:], y[:, 0:16], col(22), None, A.is_equal, None, ["yrow", "c22"], ["ohu"], 16)
    ts(cf[:, 23:25], y[:, 0:32:16], col(1), None, A.add, None, ["yrow", "cf"], ["c23"], 2)
    PRM = []
    for c in range(2):
        for k, o in enumerate((A.is_ge, A.is_gt, A.is_ge, A.is_ge)):
            a = 128 * c + 32 * k
            ts(T.prm[:, a:a + 32], y[:, 0:32], col(23 + c), 4096.0, o, A.mult, ["yrow", "c23"], ["prm%d" % a], 32)
            PRM.append("prm%d" % a)
        a = 256 + 32 * c
        ts(T.prm[:, a:a + 32], y[:, 0:32], col(23 + c), 4096.0, A.is_ge, A.mult, ["yrow", "c23"], ["prm%d" % a], 32)
        PRM.append("prm%d" % a)
    ts(T.dm[:, 0:6], y[:, 0:96:16], col(1), 2048.0, A.add, A.add, ["yrow", "cf"], ["dm"], 6)
    ts(T.cz[:], y[:, 0:240], 0.0, -1.0, A.is_ge, A.mult, ["yrow"], ["cz"], 240)
    op("V", lambda: V.memset(T.cz[:, 112:128], 0.0), [], ["cz"], vc(16))
    op("V", lambda: V.memset(T.one[:], 1.0), [], ["one"], vc(2))
    op("V", lambda: V.memset(T.ytw[:, 2048:WT], 0.0), [], ["ytd"], vc(96))
    ST0 = []
    for b in range(0, WT, 256):
        n = min(256, WT - b)
        op("S", lambda b=b, n=n: S.activation(T.st0[:, b:b + n], y[:, 0:n], F.Identity, bias=float(b)), ["yrow"], ["st0_%d" % b], vc(n))
        ST0.append("st0_%d" % b)

    me = P[r]
    sent, prev, first = [], [], {}
    for cls in sorted(set(0 if me["way"][t] == "direct" else 1 for t in range(RO) if me["way"][t] != "handed")):
        for kind, src, rd, lat in (("x", T.xo, ["xo"] + AO, 3.0), ("a", T.ao, AO, 5.0)):
            if cls == 1:
                items = [(e, src[:, 1024 * k:1024 * k + 1024], src[:, 1024 * k:1024 * k + 1024], "r" + kind)
                         for k, e in enumerate(me["helpers"])]
            else:
                t = [t for t in range(RO) if me["way"][t] == "direct"][0]
                items = [(C[me["dst"][t]], T["%sh%d" % (kind, t)][:], src[:], "b%s%d" % (kind, t))]
            tok = "sent%d%s" % (cls, kind)
            sent.append(rem(items, rd + prev, [tok], lat, 110.0 if kind == "x" else 100.0))
            first.setdefault(kind, sent[-1])
        prev = [tok]
    for t in range(RO):
        for b in range(4):
            iota(T["zt%d" % t][:, 512 * b:512 * b + 512], [[1, 8], [32, 8], [256, 8]], 8 * b, 0, ["zt%d" % t], 512)
        iota(T["zt%d" % t][:, 2048:WT], [[1, WT - 2048]], 2048, 0, ["zt%d" % t], WT - 2048)
        for b in range(4 if t else 0):
            iota(T["st%d" % t][:, 536 * b:536 * b + 536], [[1, 536]], 536 * b, 0, ["st%d" % t], 536)
    for b in range(4):
        act(T.wt[:, 536 * b:536 * b + 536], T.st0[:, 536 * b:536 * b + 536], F.Copy, ST0, ["wt"], 536)
    for t in range(RO):
        ext("bx%d" % t, ["xh%d" % t], [first["x"]], BULK[t][0])
        ext("ba%d" % t, ["ah%d" % t], [first["a"]], BULK[t][1])
    for t in range(RO - 1):
        h = (r + 1 + t % (N - 1)) % N
        if P[h]["way"][t + 1] == "handed":
            d = C[P[h]["dst"][t + 1]]
            for kind, lat in (("x", 3.0), ("a", 5.0)):
                rem([(d, T["%sh%d" % (kind, t + 1)][:], T["%sh%d" % (kind, t)][:], "b%s%d" % (kind, t + 1))], ["%sh%d" % (kind, t)], [], lat, soft=sent)

    for t in range(RO):
        L = slice(256 * t, 256 * t + 256)
        nl, jl = T.nl[:, 16 * t:16 * t + 16], T.jl[:, 16 * t:16 * t + 16]
        gat = vg if t == 0 else sg
        gat(T.xvn[:, L], T.xo[:], nl, ["xo", "nl%d" % t], ["xvn%d" % t], 256)
        sg(T.xvj[:, L], T.xo[:], jl, ["xo", "jl%d" % t], ["xvj%d" % t], 256)
        for k in range(16):
            if t == 0 and k % 3:
                cp(T.xr0[:, k::16], T.xvn[:, L], ["xvn0"], ["xr0_%d" % k], 256, 0.5)
            else:
                act(T["xr%d" % t][:, k::16], T.xvn[:, L], F.Copy, ["xvn%d" % t], ["xr%d_%d" % (t, k)], 256)
        vg(T.ownn[:, L], T.ao[:], nl, AO + ["nl%d" % t], ["ownn%d" % t], 256)
        vg(T.ownj[:, L], T.ao[:], jl, AO + ["jl%d" % t], ["ownj%d" % t], 256)
    cp(T.tgu[:], T.tgi[:], ["tgi"], ["tgu"], 128)

    def distances(t, w, win, wtok, off, o0, otok, on_s, banks, zz, ztok, late):
        dv, ab, pd, xr = T["dv" + w], T["ab" + w], T["pd" + w], T["xr%d" % t]
        XR = ["xr%d_%d" % (t, k) for k in range(16)]
        mm(pd[:, 0:256], T.idp[:], T.tb[:], True, False, ["idp", "tb"], "pd" + w, 256)
        if late is not None:
            mm(pd[:, 0:256], T.idp[:], T.tbm[:, 256 * late:256 * late + 256], False, False, ["idp", "tbm%d" % late], "pd" + w, 256)
        sp, vp = sorted(on_s), [b for b in range(8) if b not in on_s]
        pieces = []
        while sp or vp:
            if vp and (len(vp) > 1 or not sp):
                pieces.append(vp.pop(0))
            if sp:
                pieces.append(sp.pop(0))
        done = 0
        for n, b in enumerate(pieces):
            c = slice(512 * b, 512 * b + 512)
            toks = ["dv%s%d" % (w, 2 * b), "dv%s%d" % (w, 2 * b + 1)]
            atk = ["ab%s%d" % (w, 2 * b), "ab%s%d" % (w, 2 * b + 1)]
            if b in on_s:
                ps = banks[sorted(on_s).index(b) % len(banks)]
                sg(dv[:, c], win, off[:, o0 + 32 * b:o0 + 32 * b + 32], [wtok, otok], toks, 512)
                mm(T[ps][:], T.idm[:], xr[:, c], True, False, ["idm"] + XR, ps, 512)
                mm(T[ps][:], T.idp[:], dv[:, c], False, True, ["idp"] + toks, ps, 512)
                act(ab[:, c], T[ps][:], F.Abs, [ps], atk, 512)
            elif n < 7:
                vg(dv[:, c], win, off[:, o0 + 32 * b:o0 + 32 * b + 32], [wtok, otok] + XR, toks, 512, xr[:, c], A.subtract)
                act(ab[:, c], dv[:, c], F.Abs, toks, atk, 512)
            else:
                for k in range(2):
                    c2 = slice(512 * b + 256 * k, 512 * b + 256 * k + 256)
                    a = o0 + 32 * b + 16 * k
                    vg(dv[:, c2], win, off[:, a:a + 16], [wtok, otok] + XR, toks[k:k + 1], 256, xr[:, c2], A.subtract)
                    act(ab[:, c2], dv[:, c2], F.Abs, toks[k:k + 1], atk[k:k + 1], 256)
            for p in (2 * b, 2 * b + 1):
                done += 1
                mm(pd[:, 0:256], zz[:, 15 - p:143 - p], ab[:, 256 * p:256 * p + 256], False, done == 16, [ztok, "ab%s%d" % (w, p)], "pd" + w, 256)
        scan(T["ks" + w][:], T.rst[:], pd[:, 0:256], A.add, A.max, ["rst", "pd" + w], ["ks" + w], 256)

    def best(w):
        ki = T["ki" + w]
        ts(ki[:, 16:32], ki[:, 0:16], 15, None, A.bitwise_and, None, ["ki" + w], ["kj" + w], 16)
        cp(T["ku" + w][:], ki[:, 16:32], ["kj" + w], ["ku" + w], 16)

    def changes(a, kind, buf, tok):
        own, rel = upd_items(T, P, r, a, kind, buf)
        items = ([(me["helpers"]["xa".index(kind)], buf, buf, "ru%s%d" % (kind, a))] if rel else []) + own
        o = rem(items, [tok], [], 2.0)
        for (a2, b) in UPD:
            if a2 == a:
                nm = "u%s%d%d" % (kind, a, b)
                ext(nm, [nm], [o], HOP)
                if kind == "x":
                    gcopy(T["xh%d" % b][:, a::8], T[nm][:], [nm], ["xh%d" % b])
                elif b > a + 1:
                    cp(T["ah%d" % b][:, a::8], T[nm][:], [nm], ["ah%d" % b], 256)

    for t in range(RO):
        L = slice(256 * t, 256 * t + 256)
        st, zt, xh, ah = T["st%d" % t], T["zt%d" % t], T["xh%d" % t], T["ah%d" % t]
        ST, ZT, XH, AH = ["st%d" % t] if t else ST0, ["zt%d" % t], "xh%d" % t, "ah%d" % t
        tl, sl, zl, al = T.tl[:, 20 * t:20 * t + 20], T.sl[:, 4 * t:4 * t + 4], T.zl[:, 4 * t:4 * t + 4], T.al[:, 16 * t:16 * t + 16]
        TL, SL, ZL, AL, OJ = "tl%d" % t, ["sl%d_%d" % (t, k) for k in range(4)], "zl%d" % t, "al%d" % t, "ownj%d" % t
        o = 256 * t
        grp[0] = "c%d" % t
        distances(t, "c", T.xo[:], "xo", T.ownn, o, "ownn%d" % t, S_CHOICE[t], ["pr", "pb"], T.zp, "zp", None)
        grp[0] = "n%d" % t
        cp(T.kic[:, 0:16], T.ksc[:, 15::16], ["ksc"], ["kic"], 16)
        best("c")
        vg(T.mp[:, 0:32], T.ohu[:], T.kuc[:, 2:4], ["ohu", "kuc", OJ], ["mp0"], 32, T.ownj[:, o + 32:o + 64], A.mult)
        vg(T.mp[:, 32:64], T.ohu[:], T.kuc[:, 0:2], ["ohu", "kuc", OJ], ["mp1"], 32, T.ownj[:, o:o + 32], A.mult)
        vg(T.mp[:, 64:128], T.oht[:], T.kuc[:, 0:4], ["oht", "kuc", OJ], ["mp2"], 64, T.ownj[:, o:o + 64], A.mult)
        vg(T.mp[:, 128:320], T.oht[:], T.kuc[:, 4:16], ["oht", "kuc", OJ], ["mp3"], 192, T.ownj[:, o + 64:o + 256], A.mult)
        pr = T.pr
        mm(pr[:, 0:320], T.idp[:], T.prm[:], True, False, ["idp"] + PRM, "pr", 320)
        for k in range(8):
            src = T.mp[:, 64:96] if k % 2 == 0 else T.mp[:, 32:64]
            mm(pr[:, 32 * k:32 * k + 32], T.bo[:], src, False, False, ["bo", "mp1", "mp2"], "pr", 32)
        for c in range(2):
            mm(pr[:, 256 + 32 * c:288 + 32 * c], T.bo[:], T.mp[:, 96:128], False, c == 1, ["bo", "mp2"], "pr", 32)
        for p in range(16):
            mm(pr[:, 320:340], T.z1[:, 15 - p:143 - p], T.mp[:, p::16], p == 0, p == 15, ["z1", "mp0", "mp1", "mp2", "mp3"], "pr", 20)

        def pl(k):
            return pr[:, 320 + k:321 + k]
        for c in range(2):
            ts(T.ee[:, 128 * c:128 * c + 64], pr[:, 128 * c:128 * c + 64], pl(4 + c), 4096.0, A.is_equal, A.mult, ["pr"], ["ee%da" % c], 64)
            ts(T.ee[:, 128 * c + 64:128 * c + 128], pr[:, 128 * c + 64:128 * c + 128], pl(2 + c), 4096.0, A.is_equal, A.mult, ["pr"], ["ee%db" % c], 64)
        cp(tl, pr[:, 320:340], ["pr"], [TL], 20)
        for c in range(2):
            op("V", lambda c=c: V.tensor_reduce(T.pen[:, c:c + 1], T.ee[:, 128 * c:128 * c + 128], AxisListType.X, A.max),
               ["ee%da" % c, "ee%db" % c], ["pen%d" % c], vc(128))
        for c in range(2):
            ts(T.ee[:, 256 + 32 * c:288 + 32 * c], pr[:, 256 + 32 * c:288 + 32 * c], pl(6 + c), 4096.0, A.is_equal, A.mult, ["pr"], ["ee%dr" % c], 32)
            op("V", lambda c=c: V.tensor_reduce(T.pen[:, 2 + c:3 + c], T.ee[:, 256 + 32 * c:288 + 32 * c], AxisListType.X, A.max),
               ["ee%dr" % c], ["pen%d" % (2 + c)], vc(32))
        vg(T.vs[:, 0:64], zt[:], T.tl[:, 20 * t + 2:20 * t + 6], ZT + [TL], ["vz"], 64)
        vg(T.vs[:, 64:128], st[:], T.tl[:, 20 * t + 2:20 * t + 6], ST + [TL], ["vs"], 64)
        for k in range(4):
            ts(T.sl[:, 4 * t + k:4 * t + k + 1], pl((4, 5, 2, 3)[k]), T.pen[:, k % 2:k % 2 + 1], T.dm[:, k:k + 1], A.add, A.min,
               ["pr", "pen%d" % (k % 2), "dm"], [SL[k]], 1)
        for c in range(2):
            ts(T.rl[:, c:c + 1], pl(6 + c), T.pen[:, 2 + c:3 + c], T.dm[:, 4 + c:5 + c], A.add, A.min, ["pr", "pen%d" % (2 + c), "dm"], ["rl%d" % c], 1)
        vsc(zt[:], sl, T.vs[:, 0:64], SL + ["vz"], ZT, 64)
        vsc(st[:], sl, T.vs[:, 64:128], SL + ["vs"], ST, 64)
        vg(T.zz[:, 0:32], zt[:], T.rl[:], ZT + ["rl0", "rl1", "mk"], ["zza"], 32, T.mk[:], A.mult)
        vg(T.zz[:, 32:64], st[:], T.rl[:], ST + ["rl0", "rl1", "mk"], ["zzb"], 32, T.mk[:], A.mult)
        scan(T.zz[:, 64:128], T.keep[:, 0:64], T.zz[:, 0:64], A.mult, A.add, ["keep", "zza", "zzb"], ["zzs"], 64)
        cp(zl, T.zz[:, 79:128:16], ["zzs"], [ZL], 4)
        vg(T.su[:, 32 * t:32 * t + 32], st[:], T.tl[:, 20 * t:20 * t + 2], ST + [TL], ["su%d" % t], 32)
        vg(T.wt[:, L], st[:], T.tl[:, 20 * t + 4:20 * t + 20], ST + [TL], ["wt"], 256)
        vsc(T.wt[:], T.zl[:, 4 * t:4 * t + 2], T.su[:, 32 * t:32 * t + 32], [ZL, "su%d" % t], ["wt"], 32)
        tt(T.wm[:, 0:256], T.wt[:, L], T.pk[:, 0:256], A.mult, ["wt", "pk"], ["wma"], 256)
        scan(T.wm[:, 256:512], T.keep[:], T.wm[:, 0:256], A.mult, A.add, ["keep", "wma"], ["wmb"], 256)
        cp(al, T.wm[:, 271:512:16], ["wmb"], [AL], 16)
        grp[0] = "b%d" % t
        mm(pr[0:96, 0:8], T.wt[:, o + 64:o + 160], T.selp[:], True, True, ["wt", "selp"], "pr", 8, 4)
        for part, (a, b) in enumerate(PARTS):
            for w in range(8):
                ts(T.am[0:96, 256 * w + a:256 * w + b], T.ival[0:96, a:b], pr[0:96, w:w + 1], -t / 8.0, A.subtract, A.is_equal,
                   ["ival", "pr"], ["am%d_%d" % (w, part)], b - a, 0.5)
        for rnd in range(3):
            for w in range(8):
                rh = T.one[0:96, 0:1] if rnd == 0 else T.nb[0:96, w:w + 1]
                mm(T.pb[0:96, 264 + w:265 + w], T.am[0:96, 256 * w + 64:256 * w + 160], rh, True, True, ["am%d_0" % w, "one", "nb"], "pb", 1)
            if rnd < 2:
                ts(T.nb[0:96, :], T.pb[0:96, 264:272], 0.0, None, A.is_equal, None, ["pb"], ["nb"], 8)
        for w in range(8):
            ts(T.nbx[0:96, 128 * w:128 * w + 128], T.cz[0:96, 112 - 16 * w:240 - 16 * w], T.pb[0:96, 264 + w:265 + w], None, A.is_equal, None,
               ["cz", "pb"], ["nbx%d" % w], 128, 0.5)
        for w in range(8):
            mm(T.pk[:, 256:512], T.nbx[0:96, 128 * w:128 * w + 128], T.am[0:96, 256 * w:256 * w + 256], w == 0, w == 7,
               ["nbx%d" % w] + ["am%d_%d" % (w, k) for k in range(len(PARTS))], "pk", 256)
        vg(T.dd[:, 0:256], xh[:], al, [XH, AL, "xvj%d" % t], ["dda"], 256, T.xvj[:, L], A.subtract)
        ts(T.dd[:, 256:512], T.dd[:, 0:256], 1, None, A.arith_shift_right, None, ["dda"], ["ddb"], 256)
        ts(T.fr[:, L], T.pk[:, 256:512], 0.0, None, A.is_equal, None, ["pk"], ["fr%d" % t], 256)
        tt(T.fd[:], T.fr[:, L], T.dd[:, 256:512], A.mult, ["fr%d" % t, "ddb"], ["fd"], 256, 2)
        nx = T["nx%d" % t]
        if t < RO - 1:
            vg(T.xo[:, t::8], T.fd[:], T.jn[:], ["fd", "jn", "xo"], ["xo"], 256, T.xo[:, t::8], A.add)
            gcopy(nx[:], T.xo[:, t::8], ["xo"], ["nx%d" % t])
            changes(t, "x", nx[:], "nx%d" % t)
        else:
            vg(nx[:], T.fd[:], T.jn[:], ["fd", "jn", "xo"], ["nx%d" % t], 256, T.xo[:, t::8], A.add)
        dma("Y", T.yx[:, L], nx[:], ["nx%d" % t], [], 2.5)
        grp[0] = "v%d" % t
        vg(T.alj[:], ah[:], al, [AH, AL], ["alj"], 256)
        vg(T.alu[:], T.alj[:], T.tlc[:], ["alj", "tlc"], ["alu"], 256)
        distances(t, "v", xh[:], XH, T.alu, 0, "alu", S_VISIT[t], ["ps0", "ps1"], T.zm, "zm", t - 1 if t else None)
        grp[0] = "w%d" % t
        if t:
            k0 = t - 1
            cp(ah[:, k0::8], T["ua%d%d" % (k0, t)][:], ["ua%d%d" % (k0, t)], [AH], 256)
            vg(T.alf[:], ah[:], al, [AH, AL], ["alf"], 256)
            for c in range(16):
                mm(T.pq[:, 0:16], T.zk[:, 144 * k0 + 15 - c:144 * k0 + 143 - c], T.alf[:, 16 * c:16 * c + 16], c == 0, c == 15, ["zk%d" % k0, "alf"], "pq", 16)
            cp(T.lu[:], T.pq[:, 0:16], ["pq"], ["lu"], 16)
            vg(T.ld[:, 0:256], xh[:], T.lu[:], [XH, "lu", "xvn%d" % t], ["lda"], 256, T.xvn[:, L], A.subtract)
            act(T.ld[:, 256:512], T.ld[:, 0:256], F.Abs, ["lda"], ["ldb"], 256)
            mm(T.pq[:, 16:32], T.idp[:], T.tb[:, k0::16], True, False, ["idp", "tb"], "pq", 16)
            for p in range(16):
                mm(T.pq[:, 16:32], T.zm[:, 15 - p:143 - p], T.ld[:, 256 + 16 * p:272 + 16 * p], False, p == 15, ["zm", "ldb"], "pq", 16)
            tt(T.kiv[:, 0:16], T.ksv[:, 15::16], T.pq[:, 16:32], A.max, ["ksv", "pq"], ["kiv"], 16)
            alv, alt = T.alf[:], "alf"
        else:
            cp(T.kiv[:, 0:16], T.ksv[:, 15::16], ["ksv"], ["kiv"], 16)
            alv, alt = T.alj[:], "alj"
        best("v")
        vg(T.mpm[:], T.oht[:], T.kuv[:], ["oht", "kuv", alt], ["mpm"], 256, alv, A.mult)
        mm(T.pq[:, 256:512], T.dg[:, 128 * t:128 * t + 128], T.ownj[:, L], True, False, ["dg%d" % t, OJ], "pq", 256)
        mm(T.pq[:, 256:512], T.z1[:, 15 - t:143 - t], T.mpm[:], False, True, ["z1", "mpm"], "pq", 256)
        tt(T.dmv[:], T.pq[:, 256:512], T.fr[:, L], A.mult, ["pq", "fr%d" % t], ["dmv"], 256)
        no = T["no%d" % t]
        vg(no[:], T.dmv[:], T.jn[:], ["dmv", "jn"] + AO, ["no%d" % t], 256, T.ao[:, t::8], A.add)
        if t < RO - 1:
            changes(t, "a", no[:], "no%d" % t)
        dma("Y", T.ym[:, L], no[t::16, :], ["no%d" % t], [], 2.2)

    grp[0] = "yt"
    tab = T.st2
    for t in (1, 0):
        sg(T.yv[:, 256 * t:256 * t + 256], tab[:], T.al[:, 16 * t:16 * t + 16], ["st2", "al%d" % t], ["yv%d" % t], 256)
        vg(T.yc[:], tab[:], T.tl[:, 20 * t + 2:20 * t + 6], ["st2", "tl%d" % t], ["yc"], 64)
        vsc(tab[:], T.sl[:, 4 * t:4 * t + 4], T.yc[:], ["yc"] + ["sl%d_%d" % (t, k) for k in range(4)], ["st2"], 64)
        sg(T.yr[:, 32 * t:32 * t + 32], tab[:], T.tl[:, 20 * t:20 * t + 2], ["st2", "tl%d" % t], ["yr%d" % t], 32)
    YT = ["yt%d" % b for b in range(4)]
    for b in range(4):
        sg(T.ytw[:, 512 * b:512 * b + 512], tab[:], T.tgu[:, 32 * b:32 * b + 32], ["st2", "tgu"], [YT[b]], 512)
    for t in range(RO):
        win, wk = (T.yv[:, 256 * t:256 * t + 256], "yv%d" % t) if t < RO - 1 else (T.wt[:, 256 * t:256 * t + 256], "wt")
        val, vk = (T.yr[:, 32 * t:32 * t + 32], "yr%d" % t) if t < RO - 1 else (T.su[:, 32 * t:32 * t + 32], "su%d" % t)
        sg(T.ytw[:, t:2048:8], win, T.jn[:], [wk, "jn"], YT, 256)
        vsc(T.ytw[:], T.zl[:, 4 * t + 2:4 * t + 4], val, ["zl%d" % t, vk], YT + ["ytd"], 32)
    dma("Y", T.yt[:], T.ytw[0::16, 0:2048], YT, [], 2.5)
    return ops


def schedule(ops):
    lw, rs = {}, {}
    for i, o in enumerate(ops):
        d = set()
        for k in o["rd"]:
            if k in lw:
                d.add(lw[k])
            if k in BANKS:
                d.update(j for j in rs.get(k, []) if ops[j]["e"] != o["e"])
        for k in o["wr"]:
            if k in lw:
                d.add(lw[k])
            d.update(rs.get(k, []))
        d.discard(i)
        o["dep"] = sorted(d)
        for k in o["rd"]:
            rs.setdefault(k, []).append(i)
        for k in o["wr"]:
            lw[k] = i
            rs[k] = []
    n = len(ops)
    succ = [[] for _ in range(n)]
    left = [0] * n
    for i, o in enumerate(ops):
        o["all"] = sorted(set(o["dep"]) | set(o.get("soft", [])))
        left[i] = len(o["all"])
        for j in o["all"]:
            succ[j].append(i)

    def gap(j, i):
        return 0.0 if (ops[j]["e"] == "P" and ops[i]["e"] == "P") or ops[i]["e"] == "X" else SYNC
    tail = [0.0] * n
    for i in range(n - 1, -1, -1):
        tail[i] = ops[i]["c"] + ops[i]["lat"] + max([tail[k] + gap(i, k) for k in succ[i]] or [0.0])
    for i in range(n):
        tail[i] += ops[i]["boost"]
    free, at = {}, [0.0] * n
    ready = [i for i in range(n) if left[i] == 0]
    order = []
    while ready:
        st = dict((i, max(at[i], free.get(ops[i]["e"], 0.0))) for i in ready)
        i0 = min(ready, key=lambda i: (st[i], -tail[i], i))
        same = [i for i in ready if ops[i]["e"] == ops[i0]["e"] and st[i] <= st[i0] + min(0.5 * ops[i0]["c"], LOOK)]
        i = min(same, key=lambda k: (-tail[k], k))
        ready.remove(i)
        order.append(i)
        ops[i]["t0"] = st[i]
        if ops[i]["e"] != "X":
            free[ops[i]["e"]] = st[i] + ops[i]["c"]
        ops[i]["t1"] = st[i] + ops[i]["c"] + ops[i]["lat"]
        for k in succ[i]:
            at[k] = max(at[k], ops[i]["t1"] + gap(i, k))
            left[k] -= 1
            if left[k] == 0:
                ready.append(k)
    return order


def emit(g, T, ops, order):
    Q = {"V": g.vector, "S": g.scalar, "P": g.tensor, "G": g, "Y": g.sync}
    count = dict((e, 0) for e in "VSPG")
    seen = dict((e, {}) for e in Q)
    used = set(j for o in ops for j in o["dep"] if not (o["e"] == "P" and ops[j]["e"] == "P"))
    for i in order:
        o = ops[i]
        e = o["e"]
        if e == "X":
            continue
        need = {}
        for j in o["dep"]:
            if not (e == "P" and ops[j]["e"] == "P"):
                s, v = ops[j]["sem"]
                need[s] = max(need.get(s, 0), v)
        for s in sorted(need):
            if seen[e].get(s, 0) < need[s]:
                Q[e].wait_ge(T.sem[s], need[s])
                seen[e][s] = need[s]
        ins = o["fn"]()
        if "sem" not in o:
            if i in used:
                count[e] += 1
                ins.then_inc(T.sem["q" + e], 1)
            o["sem"] = ("q" + e, count[e])
    last = {}
    for o in ops:
        s, v = o["sem"]
        last[s] = max(last.get(s, 0), v)
    for s in sorted(last):
        if last[s] and seen["G"].get(s, 0) < last[s]:
            g.wait_ge(T.sem[s], last[s])


def rank_program(g, core, T, topo):
    P = plan(T, topo)
    r = T.rank_of(core)
    if r is None:
        for h in range(N):
            if core in P[h]["helpers"]:
                helper_program(g, core, T, topo, P, h, P[h]["helpers"].index(core))
        return
    ops = build(g, core, T, topo, P, r)
    emit(g, T, ops, schedule(ops))
